import numpy as np
import ml_dtypes


def mxq(x, axis, fmt="e4m3"):
    dtype, down = {"e4m3": (ml_dtypes.float8_e4m3fn, 7), "e5m2": (ml_dtypes.float8_e5m2, 14)}[fmt]
    v = np.moveaxis(np.asarray(x, np.float32).astype(ml_dtypes.bfloat16).astype(np.float64), axis, -1)
    blocks = v.reshape(v.shape[:-1] + (-1, 32))
    amax = np.abs(blocks).max(-1, keepdims=True)
    byte = np.maximum(np.where(amax > 0, np.frexp(amax)[1] - 1 + 127, 0) - down, 1)
    scale = np.exp2(byte - 127.0)
    codes = (blocks / scale).astype(np.float32).astype(dtype).astype(np.float64)
    return np.moveaxis((codes * scale).reshape(v.shape), -1, axis)


WIDE = False


def mx_kscale(k):
    if not WIDE:
        return np.ones(k)
    levels = np.array([10, -10, 5, -5, 0])
    if k % 512:
        return np.exp2(np.random.permutation(np.resize(levels, k // 32))).repeat(32)
    a = np.empty((k // 512, 16))
    for p in range(k // 512):
        a[p, :8] = np.random.permutation(np.resize(levels, 8))
        for g in range(8):
            far = levels[np.abs(levels - a[p, g]) >= 10]
            a[p, g + 8] = far[np.random.randint(len(far))]
    return np.exp2(a.ravel()).repeat(32)


BF16 = ml_dtypes.bfloat16


def bf(x):
    return np.asarray(x, np.float32).astype(BF16)


def f64(x):
    return np.asarray(x).astype(np.float64)


H, W, N = 1536, 1024, 512

STRENGTH = 0.33


def setup_inputs():
    s, u = mx_kscale(W), mx_kscale(H)
    x = np.random.standard_normal((H, W)) * u[:, None] * s
    gate = 0.5 + np.random.random((H, W))
    a = STRENGTH * np.random.standard_normal((W, W)) / np.sqrt(W) / s[:, None] * s
    b = STRENGTH * np.random.standard_normal((H, H)) / np.sqrt(H) / u
    keep = (1 + 0.1 * np.random.standard_normal(H)) / u
    p = np.random.standard_normal((W, N)) / np.sqrt(W) / s[:, None]
    return {"x": bf(x), "gate": bf(gate), "a": bf(a), "b": bf(b), "keep": bf(keep), "p": bf(p)}


def reference(x, gate, a, b, keep, p):
    x, gate, keep = f64(x), f64(gate), f64(keep)
    row_corr = mxq(x, 1, "e4m3") @ mxq(f64(a), 0, "e4m3")
    y1 = x + gate * row_corr
    col_corr = mxq(f64(b), 1, "e4m3") @ mxq(y1, 0, "e4m3")
    y2 = keep[:, None] * y1 + gate * col_corr
    return mxq(y2, 1, "e4m3") @ mxq(f64(p), 0, "e4m3")

@@ -1,0 +1,378 @@
+from collections import defaultdict
+from contextlib import ExitStack
+
+import concourse.mybir as mybir
+from concourse.masks import make_identity
+
+H, W, N = 1536, 1024, 512
+FLOPS = 2 * H * W * (W + H + N)
+
+F32 = mybir.dt.float32
+BF16 = mybir.dt.bfloat16
+U32 = mybir.dt.uint32
+U8 = mybir.dt.uint8
+FP8X4 = mybir.dt.float8_e4m3fn_x4
+MULT = mybir.AluOpType.mult
+ADD = mybir.AluOpType.add
+
+P = 128
+PACK = 4
+SPAN = P * PACK
+GROUPS = H // SPAN
+HALVES = W // SPAN
+
+LOADS = "a00 x00 a01 x01 g00 x10 x11 g10 x20 x21 g20 a10 a11 g01 b00 b01 g11 b10 g21 b11"
+MM_BANKS = 4
+XLAG = 0
+BLAG = 1
+ZLAG = 1
+TLAG = 2
+S3LAG = 1
+CASTD = 1
+CASTLAG = 1
+A_ROUND = 3
+A_LAG = 1
+B_ROUND = 5
+B_RATE = (5, 2)
+P_ROUND = 11
+AHEAD = 4
+TAIL = 1
+G_FROM = 99
+G_TO = 12
+MID = 0
+QFIRST = 1
+VEV = ()
+UPOS = 1
+Y2BUFS = 8
+TBUFS = 8
+HEADN = 3
+STAGE1 = [(0, 0), (1, 0), (2, 0), (0, 1), (1, 1), (2, 1)]
+
+
+def tile_terrain_row_column_smoothing_t1_kernel(tc, x, gate, a, b, keep, p, out):
+    nc = tc.nc
+    x_rows = x.rearrange("(g p t) w -> g p t w", p=P, t=PACK)
+    gate_rows = gate.rearrange("(g p t) w -> g p t w", p=P, t=PACK)
+    b_rows = b.rearrange("(g p t) k -> g p t k", p=P, t=PACK)
+    out_rows = out.rearrange("(g p t) n -> g p t n", p=P, t=PACK)
+    a_rows = a.rearrange("(j p r) n -> j p r n", p=P, r=PACK)
+    p_rows = p.rearrange("(j p r) n -> j p r n", p=P, r=PACK)
+
+    with ExitStack() as ctx:
+        res = ctx.enter_context(tc.tile_pool(name="res", bufs=1))
+        stage = ctx.enter_context(tc.tile_pool(name="stage", bufs=4))
+        psum = ctx.enter_context(tc.psum_pool(name="psum", bufs=1))
+        ctx.enter_context(tc.manual_schedule())
+
+        ident = res.tile([P, P], F32, name="ident")
+        make_identity(nc, ident[:])
+
+        x_sb, gate_sb, b_sb, a_sb, p_sb = {}, {}, {}, {}, {}
+        xq, aq, bq, pq, y1q, y2q = {}, {}, {}, {}, {}, {}
+        y1, y2, acc, gated = {}, {}, {}, {}
+        count = defaultdict(int)
+        later = defaultdict(list)
+        done = set()
+        pending = []
+
+        def at(slot, step, f):
+            assert (slot, step) not in done
+            later[slot, step].append(f)
+
+        def run(slot, step):
+            for f in later[slot, step]:
+                f()
+            done.add((slot, step))
+
+        def bank(ring):
+            first, size = (0, MM_BANKS) if ring == "mm" else (MM_BANKS, 8 - MM_BANKS)
+            name = "bank%d" % (first + count[ring] % size)
+            count[ring] = count[ring] + 1
+            return psum.tile([P, SPAN], F32, name=name, tag=name)
+
+        def reuse(kind, tags):
+            tag = tags[count[kind] % len(tags)]
+            count[kind] = count[kind] + 1
+            return res.tile([P, SPAN], F32, name=kind, tag=tag)
+
+        def load_x(g, h):
+            x_sb[g, h] = res.tile([P, 2, W], BF16, name="x%d%d" % (g, h), tag="x%d%d" % (g, h))
+            nc.sync.dma_start(out=x_sb[g, h][:], in_=x_rows[g][:, 2 * h : 2 * h + 2, :])
+
+        def load_gate(g, c):
+            gate_sb[g, c] = res.tile([P, PACK, SPAN], BF16, name="gate%d%d" % (g, c))
+            nc.sync.dma_start(out=gate_sb[g, c][:], in_=gate_rows[g][:, :, c * SPAN : (c + 1) * SPAN])
+
+        def load_b(g, h):
+            b_sb[g, h] = stage.tile([P, 2, H], BF16, name="b_raw", tag="b_raw", bufs=4)
+            nc.sync.dma_start(out=b_sb[g, h][:], in_=b_rows[g][:, 2 * h : 2 * h + 2, :])
+
+        def load_a(c, j):
+            a_sb[c, j] = stage.tile([P, PACK, SPAN], BF16, name="w_raw", tag="w_raw")
+            nc.sync.dma_start(out=a_sb[c, j][:], in_=a_rows[j][:, :, c * SPAN : (c + 1) * SPAN])
+
+        def load_p(j):
+            p_sb[j] = stage.tile([P, PACK, N], BF16, name="w_raw", tag="w_raw")
+            nc.sync.dma_start(out=p_sb[j][:], in_=p_rows[j])
+
+        def quantize(grouped, name):
+            width = grouped.shape[1] // PACK
+            tag, bufs = {"x": ("rows", 13), "z": ("rows", 13), "a": ("weights", 4), "p": ("weights", 4), "b": ("b", 18), "y": ("y1", 6)}[name[0]]
+            codes = res.tile([P, width], U32, name="c_" + name, tag="c_" + tag, bufs=bufs, align_bytes=64)
+            scales = res.tile([P, width], U8, name="s_" + name, tag="s_" + tag, bufs=bufs, align_bytes=64)
+            nc.vector.quantize_mx(out=codes[:].bitcast(FP8X4), scales=scales[:], in_=grouped[:])
+            return codes, scales
+
+        def wide_stage():
+            return stage.tile([P, PACK * SPAN], BF16, name="wide", tag="wide", bufs=3, align_bytes=64)
+
+        def group_a(c, j, copy):
+            grouped = wide_stage()
+            copy(
+                out=grouped[:].rearrange("p (u m e r) -> p m r u e", u=2, e=2, r=PACK),
+                in_=a_sb[c, j][:].rearrange("p r (m u e) -> p m r u e", u=2, e=2),
+            )
+            return grouped
+
+        def group_p(j):
+            grouped = wide_stage()
+            nc.scalar.copy(
+                out=grouped[:].rearrange("p (n i r) -> p n r i", i=4, r=PACK),
+                in_=p_sb[j][:].rearrange("p r (n i) -> p n r i", i=4),
+            )
+            return grouped
+
+        def turn(units):
+            turned = bank("side")
+            for i, unit in enumerate(units):
+                for u in range(2):
+                    col = (2 * i + u) * P
+                    nc.tensor.transpose(turned[:, col : col + P], unit[u], ident[:])
+            n = len(units)
+            grouped = stage.tile([P, n * SPAN], BF16, name="turned", tag="turned", bufs=TBUFS, align_bytes=64)
+            nc.scalar.copy(
+                out=grouped[:].bitcast(F32).rearrange("p (i r u) -> p i r u", i=n, u=2),
+                in_=turned[:, : n * 2 * P].rearrange("p (i u r) -> p i r u", i=n, u=2),
+            )
+            return grouped
+
+        def stepped_words(row, j):
+            words = row.bitcast(F32)
+            return [words[:, 2 * P * j + u : 2 * P * (j + 1) : 2] for u in range(2)]
+
+        def split(planes, store, keys):
+            codes, scales = planes
+            for i, key in enumerate(keys):
+                store[key] = (codes[:, i * P : (i + 1) * P], scales[:, i * P : (i + 1) * P])
+
+        def turn_job(step, units, store, keys, name, then=None, lag=None):
+            grouped = turn(units)
+
+            def finish():
+                split(quantize(grouped, name), store, keys)
+                if then is not None:
+                    then()
+
+            at("v", step + lag, finish)
+
+        def x_job(step, g, t, lag=None):
+            row = x_sb[g, t // 2][:, t % 2, :]
+            turn_job(step, [stepped_words(row, j) for j in range(HALVES)], xq, [(g, t, j) for j in range(HALVES)], "x%d%d" % (g, t), lag=lag)
+
+        b_units = [(g, t, j) for g in range(GROUPS) for t in range(PACK) for j in range(GROUPS)]
+
+        def b_job(step, i):
+            keys = b_units[2 * i : 2 * i + 2]
+            units = [stepped_words(b_sb[g, t // 2][:, t % 2, :], j) for g, t, j in keys]
+            turn_job(step, units, bq, keys, "b%d" % i, lag=BLAG)
+
+        def wide_job(step, grouped, store, key, name, lag):
+            def finish():
+                codes, scales = quantize(grouped, name)
+                store[key] = (codes[:], scales[:])
+
+            at("v", step + lag, finish)
+
+        def accumulate(dst, pairs, first=0, total=None):
+            total = total or len(pairs)
+            for i, (lhs, rhs) in enumerate(pairs):
+                nc.tensor.matmul_mx(
+                    out=dst, lhsT=lhs[0].bitcast(FP8X4), lhsT_scale=lhs[1], rhs=rhs[0].bitcast(FP8X4), rhs_scale=rhs[1],
+                    start=(first + i == 0), stop=(first + i == total - 1),
+                )
+
+        def sorted_view(ap):
+            return ap.rearrange("p (m u e) -> p u m e", u=2, e=2)
+
+        def plain_view(ap):
+            return ap.rearrange("p (u m e) -> p u m e", u=2, e=2)
+
+        def product(tile_key):
+            st, g, c, t = tile_key
+            acc[tile_key] = bank("mm")
+            if st == 1:
+                accumulate(acc[tile_key][:], [(xq[g, t, j], aq[c, j]) for j in range(HALVES)])
+            else:
+                accumulate(acc[tile_key][:], [(bq[g, t, j], y1q[j, c]) for j in range(GROUPS)])
+
+        def apply_gate(tile_key):
+            st, g, c, t = tile_key
+            if st == 1:
+                if t == 0:
+                    y1[g, c] = res.tile([P, PACK, SPAN], F32, name="y1_%d%d" % (g, c))
+                gated[tile_key] = y1[g, c][:, t, :]
+            else:
+                tmp = reuse("gated", ("x00", "x01", "x10", "x11"))
+                gated[tile_key] = tmp[:]
+            nc.vector.tensor_tensor(
+                out=plain_view(gated[tile_key]), in0=plain_view(acc[tile_key][:]), in1=sorted_view(gate_sb[g, c][:, t, :]), op=MULT
+            )
+
+        def project(rows):
+            for g, t in rows:
+                copy = nc.vector.tensor_copy if PACK * g + t in VEV else nc.scalar.copy
+                dst = bank("side")
+                accumulate(dst[:], [(y2q[g, t, j], pq[j]) for j in range(HALVES)])
+                result = stage.tile([P, N], F32, name="result", tag="b_raw", bufs=4)
+                copy(out=result[:], in_=dst[:])
+                nc.sync.dma_start(out=out_rows[g][:, t, :], in_=result[:])
+
+        def project_split(g, t):
+            half = N // 2
+            result = stage.tile([P, N], F32, name="result", tag="wide", bufs=3, align_bytes=64)
+            for i, copy in enumerate((nc.scalar.copy, nc.vector.tensor_copy)):
+                cols = slice(i * half, (i + 1) * half)
+                dst = bank("side")
+                accumulate(dst[:, :half], [(y2q[g, t, j], (pq[j][0][:, cols], pq[j][1][:, cols])) for j in range(HALVES)])
+                copy(out=result[:, cols], in_=dst[:, :half])
+            nc.sync.dma_start(out=out_rows[g][:, t, :], in_=result[:])
+
+        def turn_y2(rnd, keys, zlag, s3lag):
+            units = []
+            for g, t, c in keys:
+                words = y2[g, c, t][:].bitcast(F32)
+                units.append([words[:, :P], words[:, P:]])
+            ready = [(g, t) for g, t, c in keys if c == HALVES - 1]
+            s3 = rnd + zlag + s3lag
+            turn_job(rnd, units, y2q, keys, "z%d" % rnd, lambda: at("u", s3, lambda: project(ready)), zlag)
+
+        def combine(rnd, tile_key, eng):
+            st, g, c, t = tile_key
+            if st == 1:
+                x_part = x_sb[g, t // 2][:, t % 2, c * SPAN : (c + 1) * SPAN]
+                eng.tensor_tensor(out=plain_view(gated[tile_key]), in0=plain_view(gated[tile_key]), in1=sorted_view(x_part), op=ADD)
+                if t == PACK - 1:
+                    delay = 0 if (g, c) == STAGE1[-1] else CASTD
+
+                    def cast():
+                        grouped = wide_stage()
+                        nc.scalar.copy(
+                            out=grouped[:].rearrange("p (n i t) -> p n t i", i=2, t=PACK),
+                            in_=y1[g, c][:].rearrange("p t (n i) -> p n t i", i=2),
+                        )
+                        wide_job(rnd + delay, grouped, y1q, (g, c), "y1_%d%d" % (g, c), CASTLAG)
+
+                    at("s", rnd + delay, cast)
+            else:
+                y2[g, c, t] = stage.tile([P, SPAN], BF16, name="y2", tag="y2", bufs=Y2BUFS)
+                nc.vector.scalar_tensor_tensor(
+                    out=y2[g, c, t][:], in0=y1[g, c][:, t, :], scalar=keep_sb[:, PACK * g + t : PACK * g + t + 1],
+                    in1=gated[tile_key], op0=MULT, op1=ADD,
+                )
+
+        loaders = {"a": load_a, "x": load_x, "g": load_gate, "b": load_b}
+        for item in LOADS.split():
+            loaders[item[0]](int(item[1]), int(item[2]))
+        keep_sb = res.tile([P, GROUPS * PACK], BF16, name="keep")
+        nc.sync.dma_start(out=keep_sb[:].rearrange("p (g t) -> p g t", t=PACK), in_=keep.rearrange("(g p t) -> p g t", p=P, t=PACK))
+
+        g00 = group_a(0, 0, nc.vector.tensor_copy)
+        x_job(-4, 0, 0, 1)
+        x_job(-4, 0, 1, 3)
+        wide_job(-4, g00, aq, (0, 0), "a00", 0)
+        run("v", -4)
+        g01 = group_a(0, 1, nc.vector.tensor_copy)
+        run("v", -3)
+        wide_job(-2, g01, aq, (0, 1), "a01", 0)
+        run("v", -2)
+        run("v", -1)
+        for t in range(2, HEADN):
+            x_job(-1, 0, t, 1)
+        for t in range(HEADN, PACK):
+            at("t", 0, lambda t=t: x_job(0, 0, t, 0))
+
+        for g in range(1, GROUPS):
+            for t in range(PACK):
+                r = 2 * (g - 1) + t // 2
+                at("t", r, lambda g=g, t=t, r=r: x_job(r, g, t, XLAG))
+        for j in range(HALVES):
+            at("s", A_ROUND + j, lambda j=j: wide_job(A_ROUND + j, group_a(1, j, nc.scalar.copy), aq, (1, j), "a1%d" % j, A_LAG))
+            at("s", A_ROUND + j, lambda j=j: load_p(j))
+            at("s", P_ROUND + j, lambda j=j: wide_job(P_ROUND + j, group_p(j), pq, j, "p%d" % j, 1))
+        for i in range(len(b_units) // 2):
+            r = B_ROUND + (i * B_RATE[1]) // B_RATE[0]
+            at("t", r, lambda i=i, r=r: b_job(r, i))
+            if i in (2, 5):
+                at("s", r, lambda i=i: load_b(2, i // 3))
+
+        tiles = [(1, g, c, t) for g, c in STAGE1 for t in range(PACK)]
+        rows = [(g, t) for g in range(GROUPS) for t in range(PACK)]
+        tiles = tiles + [(2, g, c, t) for c in range(HALVES) for g, t in rows[:AHEAD]]
+        tiles = tiles + [(2, g, c, t) for g, t in rows[AHEAD:] for c in range(HALVES)]
+        rounds = len(tiles) // 2
+        product(tiles[0])
+        product(tiles[1])
+        for rnd in range(rounds - 1):
+            pair = tiles[2 * rnd : 2 * rnd + 2]
+            run("t", rnd)
+            for key in pair:
+                apply_gate(key)
+            on_pool = G_FROM <= rnd < G_TO
+            if on_pool:
+                combine(rnd, pair[1], nc.gpsimd)
+            combine(rnd, pair[0], nc.vector)
+            run("v", rnd)
+            if not on_pool:
+                combine(rnd, pair[1], nc.vector)
+            if pair[0][0] == 2:
+                keys = [(g, t, c) for st, g, c, t in pair]
+                r = min(rnd + TLAG, rounds - 1)
+                zlag = min(ZLAG, rounds - 1 - r)
+                at("m" if MID and r < rounds - 1 else "t", r, lambda r=r, keys=keys, zlag=zlag: turn_y2(r, keys, zlag, max(0, min(S3LAG, rounds - 2 - r - zlag))))
+            run("s", rnd)
+            product(tiles[2 * rnd + 2])
+            run("m", rnd)
+            product(tiles[2 * rnd + 3])
+            run("u", rnd)
+        rnd = rounds - 1
+        pair = tiles[-2:]
+        g, t = rows[-1]
+        run("t", rnd)
+        for key in pair:
+            apply_gate(key)
+        def last_turn(c):
+            words = y2[g, c, t][:].bitcast(F32)
+            return turn([[words[:, :P], words[:, P:]]])
+
+        jobs = list(later["v", rnd])
+        later["v", rnd].clear()
+        for f in jobs[:QFIRST]:
+            f()
+        for f in later["u", rnd]:
+            f()
+        later["u", rnd].clear()
+        combine(rnd, pair[0], nc.vector)
+        combine(rnd, pair[1], nc.vector)
+        for f in jobs[QFIRST:]:
+            f()
+        first = last_turn(0)
+        if UPOS == 0:
+            run("u", rnd)
+        second = last_turn(1)
+        split(quantize(first, "z_last0"), y2q, [(g, t, 0)])
+        if UPOS == 1:
+            run("u", rnd)
+        split(quantize(second, "z_last1"), y2q, [(g, t, 1)])
+        if UPOS == 2:
+            run("u", rnd)
+        project_split(g, t)

@@ -21,25 +21,31 @@ SPAN = P * PACK
 GROUPS = H // SPAN
 HALVES = W // SPAN
 
-LOADS = "a00 x00 a01 x01 g00 x10 x11 g10 x20 x21 g20 a10 a11 g01 b00 b01 g11 b10 g21 b11"
+LOADS = "a00 x00 a01 x01 g00 x10 x11 g10 x20 x21 a10 a11 g20 b00 b01 g01 b10 g11 b11 g21"
 MM_BANKS = 4
 XLAG = 0
-BLAG = 1
+BLAG = 2
 ZLAG = 1
 TLAG = 2
 S3LAG = 1
-CASTD = 1
-CASTLAG = 1
-A_ROUND = 3
+CASTD = 2
+CASTLAG = 2
+A_ROUND = 2
 A_LAG = 1
-B_ROUND = 5
-B_RATE = (5, 2)
-P_ROUND = 11
-AHEAD = 4
+B_ROUND = 6
+B_RATE = (3, 2)
+P_ROUND = 14
+AHEAD = 6
 TAIL = 1
-G_FROM = 99
+G_FROM = 1
 G_TO = 12
 MID = 0
+HQ = 0
+HSPLIT = 0
+A_V = ()
+B_EARLY = (2, 0)
+CASTD0 = 3
+X0 = 2
 QFIRST = 1
 VEV = ()
 UPOS = 1
@@ -262,7 +268,7 @@ def tile_terrain_row_column_smoothing_t1_kernel(tc, x, gate, a, b, keep, p, out)
                 x_part = x_sb[g, t // 2][:, t % 2, c * SPAN : (c + 1) * SPAN]
                 eng.tensor_tensor(out=plain_view(gated[tile_key]), in0=plain_view(gated[tile_key]), in1=sorted_view(x_part), op=ADD)
                 if t == PACK - 1:
-                    delay = 0 if (g, c) == STAGE1[-1] else CASTD
+                    delay = 0 if (g, c) == STAGE1[-1] else (CASTD if c == 1 else CASTD0)
 
                     def cast():
                         grouped = wide_stage()
@@ -289,13 +295,25 @@ def tile_terrain_row_column_smoothing_t1_kernel(tc, x, gate, a, b, keep, p, out)
         g00 = group_a(0, 0, nc.vector.tensor_copy)
         x_job(-4, 0, 0, 1)
         x_job(-4, 0, 1, 3)
-        wide_job(-4, g00, aq, (0, 0), "a00", 0)
+        wide_job(-4, g00, aq, (0, 0), "a00", HQ)
         run("v", -4)
-        g01 = group_a(0, 1, nc.vector.tensor_copy)
-        run("v", -3)
-        wide_job(-2, g01, aq, (0, 1), "a01", 0)
-        run("v", -2)
-        run("v", -1)
+        if HSPLIT:
+            run("v", -3)
+            g01 = wide_stage()
+            cut = HSPLIT
+            src = a_sb[0, 1][:].rearrange("p r (m u e) -> p m r u e", u=2, e=2)
+            dst = g01[:].rearrange("p (u m e r) -> p m r u e", u=2, e=2, r=PACK)
+            nc.scalar.copy(out=dst[:, :cut], in_=src[:, :cut])
+            nc.vector.tensor_copy(out=dst[:, cut:], in_=src[:, cut:])
+            run("v", -1)
+            wide_job(-2, g01, aq, (0, 1), "a01", 0)
+            run("v", -2)
+        else:
+            g01 = group_a(0, 1, nc.vector.tensor_copy)
+            run("v", -3)
+            wide_job(-2, g01, aq, (0, 1), "a01", 0)
+            run("v", -2)
+            run("v", -1)
         for t in range(2, HEADN):
             x_job(-1, 0, t, 1)
         for t in range(HEADN, PACK):
@@ -306,11 +324,11 @@ def tile_terrain_row_column_smoothing_t1_kernel(tc, x, gate, a, b, keep, p, out)
                 r = 2 * (g - 1) + t // 2
                 at("t", r, lambda g=g, t=t, r=r: x_job(r, g, t, XLAG))
         for j in range(HALVES):
-            at("s", A_ROUND + j, lambda j=j: wide_job(A_ROUND + j, group_a(1, j, nc.scalar.copy), aq, (1, j), "a1%d" % j, A_LAG))
+            at("s", A_ROUND + j, lambda j=j: wide_job(A_ROUND + j, group_a(1, j, nc.vector.tensor_copy if j in A_V else nc.scalar.copy), aq, (1, j), "a1%d" % j, A_LAG))
             at("s", A_ROUND + j, lambda j=j: load_p(j))
             at("s", P_ROUND + j, lambda j=j: wide_job(P_ROUND + j, group_p(j), pq, j, "p%d" % j, 1))
         for i in range(len(b_units) // 2):
-            r = B_ROUND + (i * B_RATE[1]) // B_RATE[0]
+            r = B_ROUND + (i * B_RATE[1]) // B_RATE[0] if i >= B_EARLY[1] else B_EARLY[0] + i
             at("t", r, lambda i=i, r=r: b_job(r, i))
             if i in (2, 5):
                 at("s", r, lambda i=i: load_b(2, i // 3))
@@ -320,8 +338,11 @@ def tile_terrain_row_column_smoothing_t1_kernel(tc, x, gate, a, b, keep, p, out)
         tiles = tiles + [(2, g, c, t) for c in range(HALVES) for g, t in rows[:AHEAD]]
         tiles = tiles + [(2, g, c, t) for g, t in rows[AHEAD:] for c in range(HALVES)]
         rounds = len(tiles) // 2
-        product(tiles[0])
-        product(tiles[1])
+        for key in tiles[:2]:
+            acc[key] = bank("mm")
+        for j in range(HALVES):
+            for key in tiles[:2]:
+                accumulate(acc[key][:], [(xq[0, key[3], j], aq[0, j])], j, HALVES)
         for rnd in range(rounds - 1):
             pair = tiles[2 * rnd : 2 * rnd + 2]
             run("t", rnd)

@@ -14,151 +14,125 @@ U8 = mybir.dt.uint8
 FP8X4 = mybir.dt.float8_e4m3fn_x4
 MULT = mybir.AluOpType.mult
 ADD = mybir.AluOpType.add
+COPY = mybir.ActivationFunctionType.Copy
 
 P = 128
 PACK = 4
 SPAN = P * PACK
 GROUPS = H // SPAN
 HALVES = W // SPAN
+ROW_TILES = GROUPS * PACK
+ROUNDS = ROW_TILES * HALVES
+STAGE_ROUNDS = ROUNDS // 2
+LAST = ROUNDS - 1
+RING = 4
 
-LOADS = "a00 x00 a01 x01 g00 x10 x11 g10 x20 x21 a10 a11 g20 b00 b01 g01 b10 g11 b11 g21"
-MM_BANKS = 4
-XLAG = 0
-BLAG = 2
-ZLAG = 1
-TLAG = 2
-S3LAG = 1
-CASTD = 2
-CASTLAG = 2
-A_ROUND = 2
-A_LAG = 1
-B_ROUND = 6
-B_RATE = (3, 2)
-P_ROUND = 14
+LAG = 2
+POOL_FROM = 3
+B_FROM = 3
+P_FROM = 16
 AHEAD = 6
-TAIL = 1
-G_FROM = 1
-G_TO = 12
-MID = 0
-HQ = 0
-HSPLIT = 0
-A_V = ()
-B_EARLY = (2, 0)
-CASTD0 = 3
-X0 = 2
-QFIRST = 1
-VEV = ()
-UPOS = 1
-Y2BUFS = 8
-TBUFS = 8
-HEADN = 3
-STAGE1 = [(0, 0), (1, 0), (2, 0), (0, 1), (1, 1), (2, 1)]
 
 
 def tile_terrain_row_column_smoothing_t1_kernel(tc, x, gate, a, b, keep, p, out):
     nc = tc.nc
-    x_rows = x.rearrange("(g p t) w -> g p t w", p=P, t=PACK)
-    gate_rows = gate.rearrange("(g p t) w -> g p t w", p=P, t=PACK)
-    b_rows = b.rearrange("(g p t) k -> g p t k", p=P, t=PACK)
-    out_rows = out.rearrange("(g p t) n -> g p t n", p=P, t=PACK)
-    a_rows = a.rearrange("(j p r) n -> j p r n", p=P, r=PACK)
-    p_rows = p.rearrange("(j p r) n -> j p r n", p=P, r=PACK)
+    x_rows = x.rearrange("(g q t) w -> g q t w", q=P, t=PACK)
+    gate_rows = gate.rearrange("(g q t) w -> g q t w", q=P, t=PACK)
+    b_rows = b.rearrange("(g q t) k -> g q t k", q=P, t=PACK)
+    out_rows = out.rearrange("(g q t) n -> g q t n", q=P, t=PACK)
+    a_rows = a.rearrange("(j q r) n -> j q r n", q=P, r=PACK)
+    p_rows = p.rearrange("(j q r) n -> j q r n", q=P, r=PACK)
 
     with ExitStack() as ctx:
-        res = ctx.enter_context(tc.tile_pool(name="res", bufs=1))
-        stage = ctx.enter_context(tc.tile_pool(name="stage", bufs=4))
+        sbuf = ctx.enter_context(tc.tile_pool(name="sbuf", bufs=1))
         psum = ctx.enter_context(tc.psum_pool(name="psum", bufs=1))
         ctx.enter_context(tc.manual_schedule())
 
-        ident = res.tile([P, P], F32, name="ident")
+        ident = sbuf.tile([P, P], F32, name="ident")
         make_identity(nc, ident[:])
 
         x_sb, gate_sb, b_sb, a_sb, p_sb = {}, {}, {}, {}, {}
         xq, aq, bq, pq, y1q, y2q = {}, {}, {}, {}, {}, {}
-        y1, y2, acc, gated = {}, {}, {}, {}
-        count = defaultdict(int)
-        later = defaultdict(list)
-        done = set()
-        pending = []
+        y1, y2, sums, gated = {}, {}, {}, {}
+        taken = defaultdict(int)
+        planned = defaultdict(list)
 
-        def at(slot, step, f):
-            assert (slot, step) not in done
-            later[slot, step].append(f)
+        def plan(place, rnd, step):
+            planned[place, rnd].append(step)
 
-        def run(slot, step):
-            for f in later[slot, step]:
-                f()
-            done.add((slot, step))
+        def run(place, rnd):
+            for step in planned[place, rnd]:
+                step()
 
         def bank(ring):
-            first, size = (0, MM_BANKS) if ring == "mm" else (MM_BANKS, 8 - MM_BANKS)
-            name = "bank%d" % (first + count[ring] % size)
-            count[ring] = count[ring] + 1
+            name = "%s%d" % (ring, taken[ring] % RING)
+            taken[ring] = taken[ring] + 1
             return psum.tile([P, SPAN], F32, name=name, tag=name)
 
-        def reuse(kind, tags):
-            tag = tags[count[kind] % len(tags)]
-            count[kind] = count[kind] + 1
-            return res.tile([P, SPAN], F32, name=kind, tag=tag)
 
-        def load_x(g, h):
-            x_sb[g, h] = res.tile([P, 2, W], BF16, name="x%d%d" % (g, h), tag="x%d%d" % (g, h))
-            nc.sync.dma_start(out=x_sb[g, h][:], in_=x_rows[g][:, 2 * h : 2 * h + 2, :])
+        def load_x(g, pair):
+            name = "x%d%d" % (g, pair)
+            x_sb[g, pair] = sbuf.tile([P, 2, W], BF16, name=name, tag=name)
+            nc.sync.dma_start(out=x_sb[g, pair][:], in_=x_rows[g][:, 2 * pair : 2 * pair + 2, :])
 
         def load_gate(g, c):
-            gate_sb[g, c] = res.tile([P, PACK, SPAN], BF16, name="gate%d%d" % (g, c))
+            gate_sb[g, c] = sbuf.tile([P, PACK, SPAN], BF16, name="gate%d%d" % (g, c))
             nc.sync.dma_start(out=gate_sb[g, c][:], in_=gate_rows[g][:, :, c * SPAN : (c + 1) * SPAN])
 
-        def load_b(g, h):
-            b_sb[g, h] = stage.tile([P, 2, H], BF16, name="b_raw", tag="b_raw", bufs=4)
-            nc.sync.dma_start(out=b_sb[g, h][:], in_=b_rows[g][:, 2 * h : 2 * h + 2, :])
+        def load_b(g, pair):
+            b_sb[g, pair] = sbuf.tile([P, 2, H], BF16, name="b_raw", tag="b_raw", bufs=4)
+            nc.sync.dma_start(out=b_sb[g, pair][:], in_=b_rows[g][:, 2 * pair : 2 * pair + 2, :])
 
         def load_a(c, j):
-            a_sb[c, j] = stage.tile([P, PACK, SPAN], BF16, name="w_raw", tag="w_raw")
+            a_sb[c, j] = sbuf.tile([P, PACK, SPAN], BF16, name="weight_raw", tag="weight_raw", bufs=2)
             nc.sync.dma_start(out=a_sb[c, j][:], in_=a_rows[j][:, :, c * SPAN : (c + 1) * SPAN])
 
         def load_p(j):
-            p_sb[j] = stage.tile([P, PACK, N], BF16, name="w_raw", tag="w_raw")
+            p_sb[j] = sbuf.tile([P, PACK, N], BF16, name="weight_raw", tag="weight_raw", bufs=2)
             nc.sync.dma_start(out=p_sb[j][:], in_=p_rows[j])
 
-        def quantize(grouped, name):
+
+        def quantize(grouped, tag, bufs):
             width = grouped.shape[1] // PACK
-            tag, bufs = {"x": ("rows", 13), "z": ("rows", 13), "a": ("weights", 4), "p": ("weights", 4), "b": ("b", 18), "y": ("y1", 6)}[name[0]]
-            codes = res.tile([P, width], U32, name="c_" + name, tag="c_" + tag, bufs=bufs, align_bytes=64)
-            scales = res.tile([P, width], U8, name="s_" + name, tag="s_" + tag, bufs=bufs, align_bytes=64)
+            codes = sbuf.tile([P, width], U32, name="codes", tag="codes_" + tag, bufs=bufs, align_bytes=64)
+            scales = sbuf.tile([P, width], U8, name="scales", tag="scales_" + tag, bufs=bufs, align_bytes=64)
             nc.vector.quantize_mx(out=codes[:].bitcast(FP8X4), scales=scales[:], in_=grouped[:])
             return codes, scales
 
-        def wide_stage():
-            return stage.tile([P, PACK * SPAN], BF16, name="wide", tag="wide", bufs=3, align_bytes=64)
+        def quantize_moving(grouped, store, key, tag, bufs):
+            codes, scales = quantize(grouped, tag, bufs)
+            store[key] = (codes[:], scales[:])
 
-        def group_a(c, j, copy):
-            grouped = wide_stage()
-            copy(
-                out=grouped[:].rearrange("p (u m e r) -> p m r u e", u=2, e=2, r=PACK),
-                in_=a_sb[c, j][:].rearrange("p r (m u e) -> p m r u e", u=2, e=2),
-            )
+        def quantize_stationary(grouped, store, keys, tag, bufs):
+            codes, scales = quantize(grouped, tag, bufs)
+            for i, key in enumerate(keys):
+                store[key] = (codes[:, i * P : (i + 1) * P], scales[:, i * P : (i + 1) * P])
+
+        def quantize_rows(grouped, store, keys):
+            quantize_stationary(grouped, store, keys, "rows", ROW_TILES + 1)
+
+        def quantize_weight(grouped, store, key):
+            quantize_moving(grouped, store, key, "weight", HALVES * HALVES)
+
+        def interleave(copy, rows, out_order, in_order, **sizes):
+            grouped = sbuf.tile([P, PACK * SPAN], BF16, name="grouped", tag="grouped", bufs=3, align_bytes=64)
+            copy(out=grouped[:].rearrange(out_order, r=PACK, **sizes), in_=rows.rearrange(in_order, **sizes))
             return grouped
 
-        def group_p(j):
-            grouped = wide_stage()
-            nc.scalar.copy(
-                out=grouped[:].rearrange("p (n i r) -> p n r i", i=4, r=PACK),
-                in_=p_sb[j][:].rearrange("p r (n i) -> p n r i", i=4),
-            )
-            return grouped
+        def interleave_a(copy, c, j):
+            return interleave(copy, a_sb[c, j][:], "q (u m e r) -> q m r u e", "q r (m u e) -> q m r u e", u=2, e=2)
 
-        def turn(units):
+        def turn(passes):
+            count = len(passes)
             turned = bank("side")
-            for i, unit in enumerate(units):
+            for i, words in enumerate(passes):
                 for u in range(2):
                     col = (2 * i + u) * P
-                    nc.tensor.transpose(turned[:, col : col + P], unit[u], ident[:])
-            n = len(units)
-            grouped = stage.tile([P, n * SPAN], BF16, name="turned", tag="turned", bufs=TBUFS, align_bytes=64)
+                    nc.tensor.transpose(turned[:, col : col + P], words[u], ident[:])
+            grouped = sbuf.tile([P, count * SPAN], BF16, name="turned", tag="turned", bufs=8, align_bytes=64)
             nc.scalar.copy(
-                out=grouped[:].bitcast(F32).rearrange("p (i r u) -> p i r u", i=n, u=2),
-                in_=turned[:, : n * 2 * P].rearrange("p (i u r) -> p i r u", i=n, u=2),
+                out=grouped[:].bitcast(F32).rearrange("q (i h u) -> q i h u", i=count, u=2),
+                in_=turned[:, : count * 2 * P].rearrange("q (i u h) -> q i h u", i=count, u=2),
             )
             return grouped
 
@@ -166,86 +140,122 @@ def tile_terrain_row_column_smoothing_t1_kernel(tc, x, gate, a, b, keep, p, out)
             words = row.bitcast(F32)
             return [words[:, 2 * P * j + u : 2 * P * (j + 1) : 2] for u in range(2)]
 
-        def split(planes, store, keys):
-            codes, scales = planes
-            for i, key in enumerate(keys):
-                store[key] = (codes[:, i * P : (i + 1) * P], scales[:, i * P : (i + 1) * P])
+        def sorted_words(g, t, c):
+            words = y2[g, t, c][:].bitcast(F32)
+            return [words[:, :P], words[:, P:]]
 
-        def turn_job(step, units, store, keys, name, then=None, lag=None):
-            grouped = turn(units)
-
-            def finish():
-                split(quantize(grouped, name), store, keys)
-                if then is not None:
-                    then()
-
-            at("v", step + lag, finish)
-
-        def x_job(step, g, t, lag=None):
+        def turn_x(g, t):
             row = x_sb[g, t // 2][:, t % 2, :]
-            turn_job(step, [stepped_words(row, j) for j in range(HALVES)], xq, [(g, t, j) for j in range(HALVES)], "x%d%d" % (g, t), lag=lag)
+            grouped = turn([stepped_words(row, j) for j in range(HALVES)])
+            return lambda: quantize_rows(grouped, xq, [(g, t, j) for j in range(HALVES)])
 
-        b_units = [(g, t, j) for g in range(GROUPS) for t in range(PACK) for j in range(GROUPS)]
+        def turn_b(rnd, keys):
+            grouped = turn([stepped_words(b_sb[g, t // 2][:, t % 2, :], j) for g, t, j in keys])
+            plan("quantise", rnd + LAG, lambda: quantize_stationary(grouped, bq, keys, "b", ROW_TILES * GROUPS // 2))
 
-        def b_job(step, i):
-            keys = b_units[2 * i : 2 * i + 2]
-            units = [stepped_words(b_sb[g, t // 2][:, t % 2, :], j) for g, t, j in keys]
-            turn_job(step, units, bq, keys, "b%d" % i, lag=BLAG)
+        def turn_y2(rnd, keys):
+            grouped = turn([sorted_words(*key) for key in keys])
+            ready = min(rnd + LAG, LAST)
 
-        def wide_job(step, grouped, store, key, name, lag):
             def finish():
-                codes, scales = quantize(grouped, name)
-                store[key] = (codes[:], scales[:])
+                quantize_rows(grouped, y2q, keys)
+                for g, t, c in keys:
+                    if c == HALVES - 1:
+                        plan("project", ready + 1 if ready + 1 < LAST else ready, lambda g=g, t=t: project(g, t))
 
-            at("v", step + lag, finish)
+            plan("quantise", ready, finish)
 
-        def accumulate(dst, pairs, first=0, total=None):
-            total = total or len(pairs)
-            for i, (lhs, rhs) in enumerate(pairs):
-                nc.tensor.matmul_mx(
-                    out=dst, lhsT=lhs[0].bitcast(FP8X4), lhsT_scale=lhs[1], rhs=rhs[0].bitcast(FP8X4), rhs_scale=rhs[1],
-                    start=(first + i == 0), stop=(first + i == total - 1),
-                )
+        def round_y1(rnd, g, c):
+            grouped = interleave(nc.scalar.copy, y1[g, c][:], "q (n i r) -> q n r i", "q r (n i) -> q n r i", i=2)
+            plan("quantise", rnd + LAG, lambda: quantize_moving(grouped, y1q, (g, c), "y1", GROUPS * HALVES))
 
-        def sorted_view(ap):
-            return ap.rearrange("p (m u e) -> p u m e", u=2, e=2)
+        def prepare_a(rnd, j):
+            grouped = interleave_a(nc.scalar.copy, 1, j)
+            plan("quantise", rnd + 1, lambda: quantize_weight(grouped, aq, (1, j)))
 
-        def plain_view(ap):
-            return ap.rearrange("p (u m e) -> p u m e", u=2, e=2)
+        def prepare_p(rnd, j):
+            grouped = interleave(nc.scalar.copy, p_sb[j][:], "q (n i r) -> q n r i", "q r (n i) -> q n r i", i=4)
+            plan("quantise", rnd + 1, lambda: quantize_weight(grouped, pq, j))
 
-        def product(tile_key):
-            st, g, c, t = tile_key
-            acc[tile_key] = bank("mm")
-            if st == 1:
-                accumulate(acc[tile_key][:], [(xq[g, t, j], aq[c, j]) for j in range(HALVES)])
-            else:
-                accumulate(acc[tile_key][:], [(bq[g, t, j], y1q[j, c]) for j in range(GROUPS)])
 
-        def apply_gate(tile_key):
-            st, g, c, t = tile_key
-            if st == 1:
-                if t == 0:
-                    y1[g, c] = res.tile([P, PACK, SPAN], F32, name="y1_%d%d" % (g, c))
-                gated[tile_key] = y1[g, c][:, t, :]
-            else:
-                tmp = reuse("gated", ("x00", "x01", "x10", "x11"))
-                gated[tile_key] = tmp[:]
-            nc.vector.tensor_tensor(
-                out=plain_view(gated[tile_key]), in0=plain_view(acc[tile_key][:]), in1=sorted_view(gate_sb[g, c][:, t, :]), op=MULT
+        def multiply(dst, lhs, rhs, first, last):
+            nc.tensor.matmul_mx(
+                out=dst,
+                lhsT=lhs[0].bitcast(FP8X4),
+                lhsT_scale=lhs[1],
+                rhs=rhs[0].bitcast(FP8X4),
+                rhs_scale=rhs[1],
+                start=first,
+                stop=last,
             )
 
-        def project(rows):
-            for g, t in rows:
-                copy = nc.vector.tensor_copy if PACK * g + t in VEV else nc.scalar.copy
-                dst = bank("side")
-                accumulate(dst[:], [(y2q[g, t, j], pq[j]) for j in range(HALVES)])
-                result = stage.tile([P, N], F32, name="result", tag="b_raw", bufs=4)
-                copy(out=result[:], in_=dst[:])
-                nc.sync.dma_start(out=out_rows[g][:, t, :], in_=result[:])
+        def accumulate(dst, operands):
+            for i, (lhs, rhs) in enumerate(operands):
+                multiply(dst, lhs, rhs, i == 0, i == len(operands) - 1)
 
-        def project_split(g, t):
+        def product(work):
+            stage, g, t, c = work
+            sums[work] = bank("product")
+            if stage == 1:
+                accumulate(sums[work][:], [(xq[g, t, j], aq[c, j]) for j in range(HALVES)])
+            else:
+                accumulate(sums[work][:], [(bq[g, t, j], y1q[j, c]) for j in range(GROUPS)])
+
+        def as_sorted(ap):
+            return ap.rearrange("q (m u e) -> q u m e", u=2, e=2)
+
+        def as_stored(ap):
+            return ap.rearrange("q (u m e) -> q u m e", u=2, e=2)
+
+        def apply_gate(work):
+            stage, g, t, c = work
+            if stage == 1:
+                if t == 0:
+                    y1[g, c] = sbuf.tile([P, PACK, SPAN], F32, name="y1_%d%d" % (g, c))
+                gated[work] = y1[g, c][:, t, :]
+            else:
+                slot = taken["gated"] % 4
+                taken["gated"] = taken["gated"] + 1
+                held = sbuf.tile([P, SPAN], F32, name="gated", tag="x%d%d" % divmod(slot, 2))
+                gated[work] = held[:]
+            nc.vector.tensor_tensor(
+                out=as_stored(gated[work]), in0=as_stored(sums[work][:]), in1=as_sorted(gate_sb[g, c][:, t, :]), op=MULT
+            )
+
+        def scale_by_keep(work):
+            stage, g, t, c = work
+            col = PACK * g + t
+            nc.scalar.activation(out=y1[g, c][:, t, :], in_=y1[g, c][:, t, :], func=COPY, scale=keep_f32[:, col : col + 1])
+
+        def combine(rnd, work, on_pool):
+            stage, g, t, c = work
+            if stage == 1:
+                engine = nc.gpsimd if on_pool else nc.vector
+                x_part = x_sb[g, t // 2][:, t % 2, c * SPAN : (c + 1) * SPAN]
+                engine.tensor_tensor(out=as_stored(gated[work]), in0=as_stored(gated[work]), in1=as_sorted(x_part), op=ADD)
+                if t == PACK - 1:
+                    when = rnd if rnd == STAGE_ROUNDS - 1 else rnd + LAG
+                    plan("scalar", when, lambda: round_y1(when, g, c))
+                return
+            y2[g, t, c] = sbuf.tile([P, SPAN], BF16, name="y2", tag="y2", bufs=8)
+            if on_pool:
+                nc.gpsimd.tensor_tensor(out=y2[g, t, c][:], in0=y1[g, c][:, t, :], in1=gated[work], op=ADD)
+            else:
+                col = PACK * g + t
+                nc.vector.scalar_tensor_tensor(
+                    out=y2[g, t, c][:], in0=y1[g, c][:, t, :], scalar=keep_sb[:, col : col + 1], in1=gated[work], op0=MULT, op1=ADD
+                )
+
+        def project(g, t):
+            dst = bank("side")
+            accumulate(dst[:], [(y2q[g, t, j], pq[j]) for j in range(HALVES)])
+            result = sbuf.tile([P, N], F32, name="result", tag="b_raw", bufs=4)
+            nc.scalar.copy(out=result[:], in_=dst[:])
+            nc.sync.dma_start(out=out_rows[g][:, t, :], in_=result[:])
+
+        def project_last(g, t):
             half = N // 2
-            result = stage.tile([P, N], F32, name="result", tag="wide", bufs=3, align_bytes=64)
+            result = sbuf.tile([P, N], F32, name="result", tag="grouped", bufs=3, align_bytes=64)
             for i, copy in enumerate((nc.scalar.copy, nc.vector.tensor_copy)):
                 cols = slice(i * half, (i + 1) * half)
                 dst = bank("side")
@@ -253,147 +263,100 @@ def tile_terrain_row_column_smoothing_t1_kernel(tc, x, gate, a, b, keep, p, out)
                 copy(out=result[:, cols], in_=dst[:, :half])
             nc.sync.dma_start(out=out_rows[g][:, t, :], in_=result[:])
 
-        def turn_y2(rnd, keys, zlag, s3lag):
-            units = []
-            for g, t, c in keys:
-                words = y2[g, c, t][:].bitcast(F32)
-                units.append([words[:, :P], words[:, P:]])
-            ready = [(g, t) for g, t, c in keys if c == HALVES - 1]
-            s3 = rnd + zlag + s3lag
-            turn_job(rnd, units, y2q, keys, "z%d" % rnd, lambda: at("u", s3, lambda: project(ready)), zlag)
-
-        def combine(rnd, tile_key, eng):
-            st, g, c, t = tile_key
-            if st == 1:
-                x_part = x_sb[g, t // 2][:, t % 2, c * SPAN : (c + 1) * SPAN]
-                eng.tensor_tensor(out=plain_view(gated[tile_key]), in0=plain_view(gated[tile_key]), in1=sorted_view(x_part), op=ADD)
-                if t == PACK - 1:
-                    delay = 0 if (g, c) == STAGE1[-1] else (CASTD if c == 1 else CASTD0)
-
-                    def cast():
-                        grouped = wide_stage()
-                        nc.scalar.copy(
-                            out=grouped[:].rearrange("p (n i t) -> p n t i", i=2, t=PACK),
-                            in_=y1[g, c][:].rearrange("p t (n i) -> p n t i", i=2),
-                        )
-                        wide_job(rnd + delay, grouped, y1q, (g, c), "y1_%d%d" % (g, c), CASTLAG)
-
-                    at("s", rnd + delay, cast)
-            else:
-                y2[g, c, t] = stage.tile([P, SPAN], BF16, name="y2", tag="y2", bufs=Y2BUFS)
-                nc.vector.scalar_tensor_tensor(
-                    out=y2[g, c, t][:], in0=y1[g, c][:, t, :], scalar=keep_sb[:, PACK * g + t : PACK * g + t + 1],
-                    in1=gated[tile_key], op0=MULT, op1=ADD,
-                )
-
-        loaders = {"a": load_a, "x": load_x, "g": load_gate, "b": load_b}
-        for item in LOADS.split():
-            loaders[item[0]](int(item[1]), int(item[2]))
-        keep_sb = res.tile([P, GROUPS * PACK], BF16, name="keep")
-        nc.sync.dma_start(out=keep_sb[:].rearrange("p (g t) -> p g t", t=PACK), in_=keep.rearrange("(g p t) -> p g t", p=P, t=PACK))
-
-        g00 = group_a(0, 0, nc.vector.tensor_copy)
-        x_job(-4, 0, 0, 1)
-        x_job(-4, 0, 1, 3)
-        wide_job(-4, g00, aq, (0, 0), "a00", HQ)
-        run("v", -4)
-        if HSPLIT:
-            run("v", -3)
-            g01 = wide_stage()
-            cut = HSPLIT
-            src = a_sb[0, 1][:].rearrange("p r (m u e) -> p m r u e", u=2, e=2)
-            dst = g01[:].rearrange("p (u m e r) -> p m r u e", u=2, e=2, r=PACK)
-            nc.scalar.copy(out=dst[:, :cut], in_=src[:, :cut])
-            nc.vector.tensor_copy(out=dst[:, cut:], in_=src[:, cut:])
-            run("v", -1)
-            wide_job(-2, g01, aq, (0, 1), "a01", 0)
-            run("v", -2)
-        else:
-            g01 = group_a(0, 1, nc.vector.tensor_copy)
-            run("v", -3)
-            wide_job(-2, g01, aq, (0, 1), "a01", 0)
-            run("v", -2)
-            run("v", -1)
-        for t in range(2, HEADN):
-            x_job(-1, 0, t, 1)
-        for t in range(HEADN, PACK):
-            at("t", 0, lambda t=t: x_job(0, 0, t, 0))
-
-        for g in range(1, GROUPS):
-            for t in range(PACK):
-                r = 2 * (g - 1) + t // 2
-                at("t", r, lambda g=g, t=t, r=r: x_job(r, g, t, XLAG))
-        for j in range(HALVES):
-            at("s", A_ROUND + j, lambda j=j: wide_job(A_ROUND + j, group_a(1, j, nc.vector.tensor_copy if j in A_V else nc.scalar.copy), aq, (1, j), "a1%d" % j, A_LAG))
-            at("s", A_ROUND + j, lambda j=j: load_p(j))
-            at("s", P_ROUND + j, lambda j=j: wide_job(P_ROUND + j, group_p(j), pq, j, "p%d" % j, 1))
-        for i in range(len(b_units) // 2):
-            r = B_ROUND + (i * B_RATE[1]) // B_RATE[0] if i >= B_EARLY[1] else B_EARLY[0] + i
-            at("t", r, lambda i=i, r=r: b_job(r, i))
-            if i in (2, 5):
-                at("s", r, lambda i=i: load_b(2, i // 3))
-
-        tiles = [(1, g, c, t) for g, c in STAGE1 for t in range(PACK)]
         rows = [(g, t) for g in range(GROUPS) for t in range(PACK)]
-        tiles = tiles + [(2, g, c, t) for c in range(HALVES) for g, t in rows[:AHEAD]]
-        tiles = tiles + [(2, g, c, t) for g, t in rows[AHEAD:] for c in range(HALVES)]
-        rounds = len(tiles) // 2
-        for key in tiles[:2]:
-            acc[key] = bank("mm")
-        for j in range(HALVES):
-            for key in tiles[:2]:
-                accumulate(acc[key][:], [(xq[0, key[3], j], aq[0, j])], j, HALVES)
-        for rnd in range(rounds - 1):
-            pair = tiles[2 * rnd : 2 * rnd + 2]
-            run("t", rnd)
-            for key in pair:
-                apply_gate(key)
-            on_pool = G_FROM <= rnd < G_TO
-            if on_pool:
-                combine(rnd, pair[1], nc.gpsimd)
-            combine(rnd, pair[0], nc.vector)
-            run("v", rnd)
-            if not on_pool:
-                combine(rnd, pair[1], nc.vector)
-            if pair[0][0] == 2:
-                keys = [(g, t, c) for st, g, c, t in pair]
-                r = min(rnd + TLAG, rounds - 1)
-                zlag = min(ZLAG, rounds - 1 - r)
-                at("m" if MID and r < rounds - 1 else "t", r, lambda r=r, keys=keys, zlag=zlag: turn_y2(r, keys, zlag, max(0, min(S3LAG, rounds - 2 - r - zlag))))
-            run("s", rnd)
-            product(tiles[2 * rnd + 2])
-            run("m", rnd)
-            product(tiles[2 * rnd + 3])
-            run("u", rnd)
-        rnd = rounds - 1
-        pair = tiles[-2:]
-        g, t = rows[-1]
-        run("t", rnd)
-        for key in pair:
-            apply_gate(key)
-        def last_turn(c):
-            words = y2[g, c, t][:].bitcast(F32)
-            return turn([[words[:, :P], words[:, P:]]])
+        works = [(1, g, t, c) for c in range(HALVES) for g, t in rows]
+        works = works + [(2, g, t, c) for c in range(HALVES) for g, t in rows[:AHEAD]]
+        works = works + [(2, g, t, c) for g, t in rows[AHEAD:] for c in range(HALVES)]
 
-        jobs = list(later["v", rnd])
-        later["v", rnd].clear()
-        for f in jobs[:QFIRST]:
-            f()
-        for f in later["u", rnd]:
-            f()
-        later["u", rnd].clear()
-        combine(rnd, pair[0], nc.vector)
-        combine(rnd, pair[1], nc.vector)
-        for f in jobs[QFIRST:]:
-            f()
-        first = last_turn(0)
-        if UPOS == 0:
-            run("u", rnd)
-        second = last_turn(1)
-        split(quantize(first, "z_last0"), y2q, [(g, t, 0)])
-        if UPOS == 1:
-            run("u", rnd)
-        split(quantize(second, "z_last1"), y2q, [(g, t, 1)])
-        if UPOS == 2:
-            run("u", rnd)
-        project_split(g, t)
+        load_a(0, 0)
+        load_x(0, 0)
+        load_a(0, 1)
+        load_x(0, 1)
+        load_gate(0, 0)
+        load_x(1, 0)
+        load_x(1, 1)
+        keep_sb = sbuf.tile([P, ROW_TILES], BF16, name="keep_sb")
+        nc.sync.dma_start(
+            out=keep_sb[:].rearrange("q (g t) -> q g t", t=PACK), in_=keep.rearrange("(g q t) -> q g t", q=P, t=PACK)
+        )
+        keep_f32 = sbuf.tile([P, ROW_TILES], F32, name="keep_f32")
+
+        grouped_a0 = interleave_a(nc.vector.tensor_copy, 0, 0)
+        finish_x0 = turn_x(0, 0)
+        finish_x1 = turn_x(0, 1)
+        quantize_weight(grouped_a0, aq, (0, 0))
+        grouped_a1 = interleave_a(nc.vector.tensor_copy, 0, 1)
+        finish_x0()
+        quantize_weight(grouped_a1, aq, (0, 1))
+        finish_x1()
+
+        load_a(1, 0)
+        load_gate(1, 0)
+        load_x(2, 0)
+        load_x(2, 1)
+        load_a(1, 1)
+        load_gate(2, 0)
+        load_b(0, 0)
+        load_b(0, 1)
+        for g in range(GROUPS):
+            load_gate(g, 1)
+            if g < 2:
+                load_b(1, g)
+
+        plan("quantise", 0, turn_x(0, 2))
+        for work in works[:2]:
+            sums[work] = bank("product")
+        for j in range(HALVES):
+            for work in works[:2]:
+                multiply(sums[work][:], xq[0, work[2], j], aq[0, j], j == 0, j == HALVES - 1)
+
+        for i, (g, t) in enumerate(rows[3:]):
+            rnd = max(i - 1, 0) // 2
+            plan("turn", rnd, lambda rnd=rnd, g=g, t=t: plan("quantise", rnd, turn_x(g, t)))
+        b_passes = [(g, t, j) for g, t in rows for j in range(GROUPS)]
+        for i in range(len(b_passes) // 2):
+            rnd = B_FROM + 2 * i // 3
+            plan("turn", rnd, lambda rnd=rnd, i=i: turn_b(rnd, b_passes[2 * i : 2 * i + 2]))
+        for j in range(HALVES):
+            plan("scalar", LAG * j, lambda j=j: prepare_a(LAG * j, j))
+            plan("scalar", P_FROM + LAG * j, lambda j=j: prepare_p(P_FROM + LAG * j, j))
+            plan("scalar", B_FROM + 2 * (3 * j + 2) // 3, lambda j=j: load_b(GROUPS - 1, j))
+        plan("scalar", B_FROM + 3, lambda: [load_p(j) for j in range(HALVES)])
+        plan("scalar", 2 * LAG, lambda: nc.scalar.activation(out=keep_f32[:], in_=keep_sb[:], func=COPY))
+        for rnd in range(STAGE_ROUNDS, LAST):
+            plan("keep", rnd - LAG, lambda rnd=rnd: scale_by_keep(works[2 * rnd + 1]))
+
+        for rnd in range(LAST):
+            first, second = works[2 * rnd : 2 * rnd + 2]
+            on_pool = rnd >= POOL_FROM
+            run("turn", rnd)
+            apply_gate(first)
+            apply_gate(second)
+            if on_pool:
+                combine(rnd, second, True)
+            combine(rnd, first, False)
+            run("quantise", rnd)
+            if not on_pool:
+                combine(rnd, second, False)
+            if rnd >= STAGE_ROUNDS:
+                when = min(rnd + LAG + rnd % 2, LAST)
+                keys = [first[1:], second[1:]]
+                plan("between" if when < LAST else "turn", when, lambda when=when, keys=keys: turn_y2(when, keys))
+            run("scalar", rnd)
+            run("keep", rnd)
+            product(works[2 * rnd + 2])
+            run("between", rnd)
+            product(works[2 * rnd + 3])
+            run("project", rnd)
+
+        run("turn", LAST)
+        for work in works[-2:]:
+            apply_gate(work)
+        for work in works[-2:]:
+            combine(LAST, work, False)
+        run("quantise", LAST)
+        halves = [turn([sorted_words(*work[1:])]) for work in works[-2:]]
+        quantize_rows(halves[0], y2q, [works[-2][1:]])
+        run("project", LAST)
+        quantize_rows(halves[1], y2q, [works[-1][1:]])
+        project_last(*rows[-1])

@@ -30,6 +30,7 @@ RING = 4
 LAG = 2
 POOL_FROM = 3
 B_FROM = 3
+B_LAG = 3
 P_FROM = 16
 AHEAD = 6
 
@@ -122,19 +123,22 @@ def tile_terrain_row_column_smoothing_t1_kernel(tc, x, gate, a, b, keep, p, out)
         def interleave_a(copy, c, j):
             return interleave(copy, a_sb[c, j][:], "q (u m e r) -> q m r u e", "q r (m u e) -> q m r u e", u=2, e=2)
 
-        def turn(passes):
+        def turn(passes, tag, bufs):
             count = len(passes)
             turned = bank("side")
             for i, words in enumerate(passes):
                 for u in range(2):
                     col = (2 * i + u) * P
                     nc.tensor.transpose(turned[:, col : col + P], words[u], ident[:])
-            grouped = sbuf.tile([P, count * SPAN], BF16, name="turned", tag="turned", bufs=8, align_bytes=64)
+            grouped = sbuf.tile([P, count * SPAN], BF16, name="turned", tag=tag, bufs=bufs, align_bytes=64)
             nc.scalar.copy(
                 out=grouped[:].bitcast(F32).rearrange("q (i h u) -> q i h u", i=count, u=2),
                 in_=turned[:, : count * 2 * P].rearrange("q (i u h) -> q i h u", i=count, u=2),
             )
             return grouped
+
+        def turn_soon(passes):
+            return turn(passes, "turned", 8)
 
         def stepped_words(row, j):
             words = row.bitcast(F32)
@@ -146,27 +150,35 @@ def tile_terrain_row_column_smoothing_t1_kernel(tc, x, gate, a, b, keep, p, out)
 
         def turn_x(g, t):
             row = x_sb[g, t // 2][:, t % 2, :]
-            grouped = turn([stepped_words(row, j) for j in range(HALVES)])
+            grouped = turn_soon([stepped_words(row, j) for j in range(HALVES)])
             return lambda: quantize_rows(grouped, xq, [(g, t, j) for j in range(HALVES)])
 
         def turn_b(rnd, keys):
-            grouped = turn([stepped_words(b_sb[g, t // 2][:, t % 2, :], j) for g, t, j in keys])
-            plan("quantise", rnd + LAG, lambda: quantize_stationary(grouped, bq, keys, "b", ROW_TILES * GROUPS // 2))
+            passes = [stepped_words(b_sb[g, t // 2][:, t % 2, :], j) for g, t, j in keys]
+            if rnd < STAGE_ROUNDS:
+                grouped = turn_soon(passes)
+                when = rnd + B_LAG
+            else:
+                grouped = turn(passes, "held", 4)
+                when = STAGE_ROUNDS - 1 + PACK * keys[0][0] + keys[0][1] - LAG
+            plan("quantise", when, lambda: quantize_stationary(grouped, bq, keys, "b", ROW_TILES * GROUPS // 2))
 
-        def turn_y2(rnd, keys):
-            grouped = turn([sorted_words(*key) for key in keys])
-            ready = min(rnd + LAG, LAST)
+        def turn_y2(keys):
+            return turn_soon([sorted_words(*key) for key in keys])
+
+        def turn_y2_in_round(rnd, keys):
+            grouped = turn_y2(keys)
 
             def finish():
                 quantize_rows(grouped, y2q, keys)
                 for g, t, c in keys:
                     if c == HALVES - 1:
-                        plan("project", ready + 1 if ready + 1 < LAST else ready, lambda g=g, t=t: project(g, t))
+                        plan("project", min(rnd + LAG, LAST), lambda g=g, t=t: project(g, t))
 
-            plan("quantise", ready, finish)
+            plan("quantise", rnd + 1, finish)
 
         def round_y1(rnd, g, c):
-            grouped = interleave(nc.scalar.copy, y1[g, c][:], "q (n i r) -> q n r i", "q r (n i) -> q n r i", i=2)
+            grouped = interleave(nc.scalar.copy, y1[g, c][:], "q (n i r) -> q n r i", "q r (n i) -> q n r i", i=4)
             plan("quantise", rnd + LAG, lambda: quantize_moving(grouped, y1q, (g, c), "y1", GROUPS * HALVES))
 
         def prepare_a(rnd, j):
@@ -326,6 +338,7 @@ def tile_terrain_row_column_smoothing_t1_kernel(tc, x, gate, a, b, keep, p, out)
         for rnd in range(STAGE_ROUNDS, LAST):
             plan("keep", rnd - LAG, lambda rnd=rnd: scale_by_keep(works[2 * rnd + 1]))
 
+        left_over = []
         for rnd in range(LAST):
             first, second = works[2 * rnd : 2 * rnd + 2]
             on_pool = rnd >= POOL_FROM
@@ -339,9 +352,12 @@ def tile_terrain_row_column_smoothing_t1_kernel(tc, x, gate, a, b, keep, p, out)
             if not on_pool:
                 combine(rnd, second, False)
             if rnd >= STAGE_ROUNDS:
-                when = min(rnd + LAG + rnd % 2, LAST)
+                when = rnd + LAG + rnd % 2
                 keys = [first[1:], second[1:]]
-                plan("between" if when < LAST else "turn", when, lambda when=when, keys=keys: turn_y2(when, keys))
+                if when < LAST:
+                    plan("between", when, lambda when=when, keys=keys: turn_y2_in_round(when, keys))
+                else:
+                    left_over.append(keys)
             run("scalar", rnd)
             run("keep", rnd)
             product(works[2 * rnd + 2])
@@ -349,14 +365,18 @@ def tile_terrain_row_column_smoothing_t1_kernel(tc, x, gate, a, b, keep, p, out)
             product(works[2 * rnd + 3])
             run("project", rnd)
 
-        run("turn", LAST)
+        turned_late = [turn_y2(keys) for keys in left_over]
         for work in works[-2:]:
             apply_gate(work)
+        run("quantise", LAST)
+        run("project", LAST)
         for work in works[-2:]:
             combine(LAST, work, False)
-        run("quantise", LAST)
-        halves = [turn([sorted_words(*work[1:])]) for work in works[-2:]]
-        quantize_rows(halves[0], y2q, [works[-2][1:]])
-        run("project", LAST)
-        quantize_rows(halves[1], y2q, [works[-1][1:]])
+        for grouped, keys in zip(turned_late, left_over):
+            quantize_rows(grouped, y2q, keys)
+        halves = [turn_y2([work[1:]]) for work in works[-2:]]
+        for grouped, work in zip(halves, works[-2:]):
+            quantize_rows(grouped, y2q, [work[1:]])
+        for keys in left_over:
+            project(*keys[0][:2])
         project_last(*rows[-1])

from collections import defaultdict
from contextlib import ExitStack

import concourse.mybir as mybir
from concourse.masks import make_identity

H, W, N = 1536, 1024, 512
FLOPS = 2 * H * W * (W + H + N)

F32 = mybir.dt.float32
BF16 = mybir.dt.bfloat16
U32 = mybir.dt.uint32
U8 = mybir.dt.uint8
FP8X4 = mybir.dt.float8_e4m3fn_x4
MULT = mybir.AluOpType.mult
ADD = mybir.AluOpType.add
COPY = mybir.ActivationFunctionType.Copy

P = 128
PACK = 4
SPAN = P * PACK
GROUPS = H // SPAN
HALVES = W // SPAN
ROW_TILES = GROUPS * PACK
ROUNDS = ROW_TILES * HALVES
STAGE_ROUNDS = ROUNDS // 2
LAST = ROUNDS - 1
RING = 4

LAG = 2
POOL_FROM = 3
B_FROM = 3
B_LAG = 3
P_FROM = 16
AHEAD = 6


def tile_terrain_row_column_smoothing_t1_kernel(tc, x, gate, a, b, keep, p, out):
    nc = tc.nc
    x_rows = x.rearrange("(g q t) w -> g q t w", q=P, t=PACK)
    gate_rows = gate.rearrange("(g q t) w -> g q t w", q=P, t=PACK)
    b_rows = b.rearrange("(g q t) k -> g q t k", q=P, t=PACK)
    out_rows = out.rearrange("(g q t) n -> g q t n", q=P, t=PACK)
    a_rows = a.rearrange("(j q r) n -> j q r n", q=P, r=PACK)
    p_rows = p.rearrange("(j q r) n -> j q r n", q=P, r=PACK)

    with ExitStack() as ctx:
        sbuf = ctx.enter_context(tc.tile_pool(name="sbuf", bufs=1))
        psum = ctx.enter_context(tc.psum_pool(name="psum", bufs=1))
        ctx.enter_context(tc.manual_schedule())

        ident = sbuf.tile([P, P], F32, name="ident")
        make_identity(nc, ident[:])

        x_sb, gate_sb, b_sb, a_sb, p_sb = {}, {}, {}, {}, {}
        xq, aq, bq, pq, y1q, y2q = {}, {}, {}, {}, {}, {}
        y1, y2, sums, gated = {}, {}, {}, {}
        taken = defaultdict(int)
        planned = defaultdict(list)

        def plan(place, rnd, step):
            planned[place, rnd].append(step)

        def run(place, rnd):
            for step in planned[place, rnd]:
                step()

        def bank(ring):
            name = "%s%d" % (ring, taken[ring] % RING)
            taken[ring] = taken[ring] + 1
            return psum.tile([P, SPAN], F32, name=name, tag=name)


        def load_x(g, pair):
            name = "x%d%d" % (g, pair)
            x_sb[g, pair] = sbuf.tile([P, 2, W], BF16, name=name, tag=name)
            nc.sync.dma_start(out=x_sb[g, pair][:], in_=x_rows[g][:, 2 * pair : 2 * pair + 2, :])

        def load_gate(g, c):
            gate_sb[g, c] = sbuf.tile([P, PACK, SPAN], BF16, name="gate%d%d" % (g, c))
            nc.sync.dma_start(out=gate_sb[g, c][:], in_=gate_rows[g][:, :, c * SPAN : (c + 1) * SPAN])

        def load_b(g, pair):
            b_sb[g, pair] = sbuf.tile([P, 2, H], BF16, name="b_raw", tag="b_raw", bufs=4)
            nc.sync.dma_start(out=b_sb[g, pair][:], in_=b_rows[g][:, 2 * pair : 2 * pair + 2, :])

        def load_a(c, j):
            a_sb[c, j] = sbuf.tile([P, PACK, SPAN], BF16, name="weight_raw", tag="weight_raw", bufs=2)
            nc.sync.dma_start(out=a_sb[c, j][:], in_=a_rows[j][:, :, c * SPAN : (c + 1) * SPAN])

        def load_p(j):
            p_sb[j] = sbuf.tile([P, PACK, N], BF16, name="weight_raw", tag="weight_raw", bufs=2)
            nc.sync.dma_start(out=p_sb[j][:], in_=p_rows[j])


        def quantize(grouped, tag, bufs):
            width = grouped.shape[1] // PACK
            codes = sbuf.tile([P, width], U32, name="codes", tag="codes_" + tag, bufs=bufs, align_bytes=64)
            scales = sbuf.tile([P, width], U8, name="scales", tag="scales_" + tag, bufs=bufs, align_bytes=64)
            nc.vector.quantize_mx(out=codes[:].bitcast(FP8X4), scales=scales[:], in_=grouped[:])
            return codes, scales

        def quantize_moving(grouped, store, key, tag, bufs):
            codes, scales = quantize(grouped, tag, bufs)
            store[key] = (codes[:], scales[:])

        def quantize_stationary(grouped, store, keys, tag, bufs):
            codes, scales = quantize(grouped, tag, bufs)
            for i, key in enumerate(keys):
                store[key] = (codes[:, i * P : (i + 1) * P], scales[:, i * P : (i + 1) * P])

        def quantize_rows(grouped, store, keys):
            quantize_stationary(grouped, store, keys, "rows", ROW_TILES + 1)

        def quantize_weight(grouped, store, key):
            quantize_moving(grouped, store, key, "weight", HALVES * HALVES)

        def interleave(copy, rows, out_order, in_order, **sizes):
            grouped = sbuf.tile([P, PACK * SPAN], BF16, name="grouped", tag="grouped", bufs=3, align_bytes=64)
            copy(out=grouped[:].rearrange(out_order, r=PACK, **sizes), in_=rows.rearrange(in_order, **sizes))
            return grouped

        def interleave_a(copy, c, j):
            return interleave(copy, a_sb[c, j][:], "q (u m e r) -> q m r u e", "q r (m u e) -> q m r u e", u=2, e=2)

        def turn(passes, tag, bufs):
            count = len(passes)
            turned = bank("side")
            for i, words in enumerate(passes):
                for u in range(2):
                    col = (2 * i + u) * P
                    nc.tensor.transpose(turned[:, col : col + P], words[u], ident[:])
            grouped = sbuf.tile([P, count * SPAN], BF16, name="turned", tag=tag, bufs=bufs, align_bytes=64)
            nc.scalar.copy(
                out=grouped[:].bitcast(F32).rearrange("q (i h u) -> q i h u", i=count, u=2),
                in_=turned[:, : count * 2 * P].rearrange("q (i u h) -> q i h u", i=count, u=2),
            )
            return grouped

        def turn_soon(passes):
            return turn(passes, "turned", 8)

        def stepped_words(row, j):
            words = row.bitcast(F32)
            return [words[:, 2 * P * j + u : 2 * P * (j + 1) : 2] for u in range(2)]

        def sorted_words(g, t, c):
            words = y2[g, t, c][:].bitcast(F32)
            return [words[:, :P], words[:, P:]]

        def turn_x(g, t):
            row = x_sb[g, t // 2][:, t % 2, :]
            grouped = turn_soon([stepped_words(row, j) for j in range(HALVES)])
            return lambda: quantize_rows(grouped, xq, [(g, t, j) for j in range(HALVES)])

        def turn_b(rnd, keys):
            passes = [stepped_words(b_sb[g, t // 2][:, t % 2, :], j) for g, t, j in keys]
            if rnd < STAGE_ROUNDS:
                grouped = turn_soon(passes)
                when = rnd + B_LAG
            else:
                grouped = turn(passes, "held", 4)
                when = STAGE_ROUNDS - 1 + PACK * keys[0][0] + keys[0][1] - LAG
            plan("quantise", when, lambda: quantize_stationary(grouped, bq, keys, "b", ROW_TILES * GROUPS // 2))

        def turn_y2(keys):
            return turn_soon([sorted_words(*key) for key in keys])

        def turn_y2_in_round(rnd, keys):
            grouped = turn_y2(keys)

            def finish():
                quantize_rows(grouped, y2q, keys)
                for g, t, c in keys:
                    if c == HALVES - 1:
                        plan("project", min(rnd + LAG, LAST), lambda g=g, t=t: project(g, t))

            plan("quantise", rnd + 1, finish)

        def round_y1(rnd, g, c):
            grouped = interleave(nc.scalar.copy, y1[g, c][:], "q (n i r) -> q n r i", "q r (n i) -> q n r i", i=4)
            plan("quantise", rnd + LAG, lambda: quantize_moving(grouped, y1q, (g, c), "y1", GROUPS * HALVES))

        def prepare_a(rnd, j):
            grouped = interleave_a(nc.scalar.copy, 1, j)
            plan("quantise", rnd + 1, lambda: quantize_weight(grouped, aq, (1, j)))

        def prepare_p(rnd, j):
            grouped = interleave(nc.scalar.copy, p_sb[j][:], "q (n i r) -> q n r i", "q r (n i) -> q n r i", i=4)
            plan("quantise", rnd + 1, lambda: quantize_weight(grouped, pq, j))


        def multiply(dst, lhs, rhs, first, last):
            nc.tensor.matmul_mx(
                out=dst,
                lhsT=lhs[0].bitcast(FP8X4),
                lhsT_scale=lhs[1],
                rhs=rhs[0].bitcast(FP8X4),
                rhs_scale=rhs[1],
                start=first,
                stop=last,
            )

        def accumulate(dst, operands):
            for i, (lhs, rhs) in enumerate(operands):
                multiply(dst, lhs, rhs, i == 0, i == len(operands) - 1)

        def product(work):
            stage, g, t, c = work
            sums[work] = bank("product")
            if stage == 1:
                accumulate(sums[work][:], [(xq[g, t, j], aq[c, j]) for j in range(HALVES)])
            else:
                accumulate(sums[work][:], [(bq[g, t, j], y1q[j, c]) for j in range(GROUPS)])

        def as_sorted(ap):
            return ap.rearrange("q (m u e) -> q u m e", u=2, e=2)

        def as_stored(ap):
            return ap.rearrange("q (u m e) -> q u m e", u=2, e=2)

        def apply_gate(work):
            stage, g, t, c = work
            if stage == 1:
                if t == 0:
                    y1[g, c] = sbuf.tile([P, PACK, SPAN], F32, name="y1_%d%d" % (g, c))
                gated[work] = y1[g, c][:, t, :]
            else:
                slot = taken["gated"] % 4
                taken["gated"] = taken["gated"] + 1
                held = sbuf.tile([P, SPAN], F32, name="gated", tag="x%d%d" % divmod(slot, 2))
                gated[work] = held[:]
            nc.vector.tensor_tensor(
                out=as_stored(gated[work]), in0=as_stored(sums[work][:]), in1=as_sorted(gate_sb[g, c][:, t, :]), op=MULT
            )

        def scale_by_keep(work):
            stage, g, t, c = work
            col = PACK * g + t
            nc.scalar.activation(out=y1[g, c][:, t, :], in_=y1[g, c][:, t, :], func=COPY, scale=keep_f32[:, col : col + 1])

        def combine(rnd, work, on_pool):
            stage, g, t, c = work
            if stage == 1:
                engine = nc.gpsimd if on_pool else nc.vector
                x_part = x_sb[g, t // 2][:, t % 2, c * SPAN : (c + 1) * SPAN]
                engine.tensor_tensor(out=as_stored(gated[work]), in0=as_stored(gated[work]), in1=as_sorted(x_part), op=ADD)
                if t == PACK - 1:
                    when = rnd if rnd == STAGE_ROUNDS - 1 else rnd + LAG
                    plan("scalar", when, lambda: round_y1(when, g, c))
                return
            y2[g, t, c] = sbuf.tile([P, SPAN], BF16, name="y2", tag="y2", bufs=8)
            if on_pool:
                nc.gpsimd.tensor_tensor(out=y2[g, t, c][:], in0=y1[g, c][:, t, :], in1=gated[work], op=ADD)
            else:
                col = PACK * g + t
                nc.vector.scalar_tensor_tensor(
                    out=y2[g, t, c][:], in0=y1[g, c][:, t, :], scalar=keep_sb[:, col : col + 1], in1=gated[work], op0=MULT, op1=ADD
                )

        def project(g, t):
            dst = bank("side")
            accumulate(dst[:], [(y2q[g, t, j], pq[j]) for j in range(HALVES)])
            result = sbuf.tile([P, N], F32, name="result", tag="b_raw", bufs=4)
            nc.scalar.copy(out=result[:], in_=dst[:])
            nc.sync.dma_start(out=out_rows[g][:, t, :], in_=result[:])

        def project_last(g, t):
            half = N // 2
            result = sbuf.tile([P, N], F32, name="result", tag="grouped", bufs=3, align_bytes=64)
            for i, copy in enumerate((nc.scalar.copy, nc.vector.tensor_copy)):
                cols = slice(i * half, (i + 1) * half)
                dst = bank("side")
                accumulate(dst[:, :half], [(y2q[g, t, j], (pq[j][0][:, cols], pq[j][1][:, cols])) for j in range(HALVES)])
                copy(out=result[:, cols], in_=dst[:, :half])
            nc.sync.dma_start(out=out_rows[g][:, t, :], in_=result[:])

        rows = [(g, t) for g in range(GROUPS) for t in range(PACK)]
        works = [(1, g, t, c) for c in range(HALVES) for g, t in rows]
        works = works + [(2, g, t, c) for c in range(HALVES) for g, t in rows[:AHEAD]]
        works = works + [(2, g, t, c) for g, t in rows[AHEAD:] for c in range(HALVES)]

        load_a(0, 0)
        load_x(0, 0)
        load_a(0, 1)
        load_x(0, 1)
        load_gate(0, 0)
        load_x(1, 0)
        load_x(1, 1)
        keep_sb = sbuf.tile([P, ROW_TILES], BF16, name="keep_sb")
        nc.sync.dma_start(
            out=keep_sb[:].rearrange("q (g t) -> q g t", t=PACK), in_=keep.rearrange("(g q t) -> q g t", q=P, t=PACK)
        )
        keep_f32 = sbuf.tile([P, ROW_TILES], F32, name="keep_f32")

        grouped_a0 = interleave_a(nc.vector.tensor_copy, 0, 0)
        finish_x0 = turn_x(0, 0)
        finish_x1 = turn_x(0, 1)
        quantize_weight(grouped_a0, aq, (0, 0))
        grouped_a1 = interleave_a(nc.vector.tensor_copy, 0, 1)
        finish_x0()
        quantize_weight(grouped_a1, aq, (0, 1))
        finish_x1()

        load_a(1, 0)
        load_gate(1, 0)
        load_x(2, 0)
        load_x(2, 1)
        load_a(1, 1)
        load_gate(2, 0)
        load_b(0, 0)
        load_b(0, 1)
        for g in range(GROUPS):
            load_gate(g, 1)
            if g < 2:
                load_b(1, g)

        plan("quantise", 0, turn_x(0, 2))
        for work in works[:2]:
            sums[work] = bank("product")
        for j in range(HALVES):
            for work in works[:2]:
                multiply(sums[work][:], xq[0, work[2], j], aq[0, j], j == 0, j == HALVES - 1)

        for i, (g, t) in enumerate(rows[3:]):
            rnd = max(i - 1, 0) // 2
            plan("turn", rnd, lambda rnd=rnd, g=g, t=t: plan("quantise", rnd, turn_x(g, t)))
        b_passes = [(g, t, j) for g, t in rows for j in range(GROUPS)]
        for i in range(len(b_passes) // 2):
            rnd = B_FROM + 2 * i // 3
            plan("turn", rnd, lambda rnd=rnd, i=i: turn_b(rnd, b_passes[2 * i : 2 * i + 2]))
        for j in range(HALVES):
            plan("scalar", LAG * j, lambda j=j: prepare_a(LAG * j, j))
            plan("scalar", P_FROM + LAG * j, lambda j=j: prepare_p(P_FROM + LAG * j, j))
            plan("scalar", B_FROM + 2 * (3 * j + 2) // 3, lambda j=j: load_b(GROUPS - 1, j))
        plan("scalar", B_FROM + 3, lambda: [load_p(j) for j in range(HALVES)])
        plan("scalar", 2 * LAG, lambda: nc.scalar.activation(out=keep_f32[:], in_=keep_sb[:], func=COPY))
        for rnd in range(STAGE_ROUNDS, LAST):
            plan("keep", rnd - LAG, lambda rnd=rnd: scale_by_keep(works[2 * rnd + 1]))

        left_over = []
        for rnd in range(LAST):
            first, second = works[2 * rnd : 2 * rnd + 2]
            on_pool = rnd >= POOL_FROM
            run("turn", rnd)
            apply_gate(first)
            apply_gate(second)
            if on_pool:
                combine(rnd, second, True)
            combine(rnd, first, False)
            run("quantise", rnd)
            if not on_pool:
                combine(rnd, second, False)
            if rnd >= STAGE_ROUNDS:
                when = rnd + LAG + rnd % 2
                keys = [first[1:], second[1:]]
                if when < LAST:
                    plan("between", when, lambda when=when, keys=keys: turn_y2_in_round(when, keys))
                else:
                    left_over.append(keys)
            run("scalar", rnd)
            run("keep", rnd)
            product(works[2 * rnd + 2])
            run("between", rnd)
            product(works[2 * rnd + 3])
            run("project", rnd)

        turned_late = [turn_y2(keys) for keys in left_over]
        for work in works[-2:]:
            apply_gate(work)
        run("quantise", LAST)
        run("project", LAST)
        for work in works[-2:]:
            combine(LAST, work, False)
        for grouped, keys in zip(turned_late, left_over):
            quantize_rows(grouped, y2q, keys)
        halves = [turn_y2([work[1:]]) for work in works[-2:]]
        for grouped, work in zip(halves, works[-2:]):
            quantize_rows(grouped, y2q, [work[1:]])
        for keys in left_over:
            project(*keys[0][:2])
        project_last(*rows[-1])
